import numpy as np
import ml_dtypes


def mxq(x, axis, fmt="e4m3"):
    dtype, down = {"e4m3": (ml_dtypes.float8_e4m3fn, 7), "e5m2": (ml_dtypes.float8_e5m2, 14)}[fmt]
    v = np.moveaxis(np.asarray(x, np.float32).astype(ml_dtypes.bfloat16).astype(np.float64), axis, -1)
    blocks = v.reshape(v.shape[:-1] + (-1, 32))
    amax = np.abs(blocks).max(-1, keepdims=True)
    byte = np.maximum(np.where(amax > 0, np.frexp(amax)[1] - 1 + 127, 0) - down, 1)
    scale = np.exp2(byte - 127.0)
    codes = (blocks / scale).astype(np.float32).astype(dtype).astype(np.float64)
    return np.moveaxis((codes * scale).reshape(v.shape), -1, axis)


WIDE = False


def mx_kscale(k):
    if not WIDE:
        return np.ones(k)
    levels = np.array([10, -10, 5, -5, 0])
    if k % 512:
        return np.exp2(np.random.permutation(np.resize(levels, k // 32))).repeat(32)
    a = np.empty((k // 512, 16))
    for p in range(k // 512):
        a[p, :8] = np.random.permutation(np.resize(levels, 8))
        for g in range(8):
            far = levels[np.abs(levels - a[p, g]) >= 10]
            a[p, g + 8] = far[np.random.randint(len(far))]
    return np.exp2(a.ravel()).repeat(32)


def f64(x):
    return np.asarray(x).astype(np.float64)


def striped(idx):
    return np.tile(idx.reshape(-1, 16).T, (8, 1)).astype(np.uint16)


def unstriped(offs):
    return offs[:16].T.reshape(-1).astype(np.int64)


def relu(v):
    return np.maximum(v, 0.0)


K, T, E, C, N = 1024, 512, 4, 256, 384


def by_expert(wq, xq):
    return np.concatenate([wq[e].T @ xq[:, e * C:(e + 1) * C] for e in range(E)], axis=1)


def setup_inputs():
    n = np.random.standard_normal
    s = mx_kscale(K)[:, None]
    first = np.random.permutation(np.repeat(np.arange(E), T // E))
    second = (first + 1 + np.random.permutation(np.repeat(np.arange(E - 1), -(-T // (E - 1)))[:T])) % E
    while np.bincount(second, minlength=E).max() != T // E:
        load = np.bincount(second, minlength=E); hi, lo = int(load.argmax()), int(load.argmin())
        t = np.flatnonzero((second == hi) & (first != lo))[0]; second[t] = lo
    slot_token = np.empty(E * C, np.int64); pos = np.empty((2, T), np.int64); fill = np.zeros(E, np.int64)
    place = np.stack([np.random.permutation(C) for _ in range(E)])
    for r, deal in enumerate((first, second)):
        for t in np.random.permutation(T):
            e = deal[t]; j = e * C + place[e, fill[e]]; fill[e] += 1; slot_token[j] = t; pos[r, t] = j
    g = np.random.uniform(0.2, 0.8, T)
    return {
        "xT": (n((K, T)) * s).astype(np.float32),
        "w": (n((E + 1, K, N)) / np.sqrt(K) / s[None]).astype(np.float32),
        "b": (0.3 * n((N, E + 1))).astype(np.float32),
        "gate": np.stack([np.tile(g, (N, 1)), np.tile(1.0 - g, (N, 1))]).astype(np.float32),
        "offs": striped(slot_token),
        "pos1": striped(pos[0]),
        "pos2": striped(pos[1]),
    }


def reference(xT, w, b, gate, offs, pos1, pos2):
    idx = unstriped(offs)
    wq = mxq(f64(w), 1, "e4m3")
    xs = mxq(f64(xT), 0, "e4m3")
    ys = relu((wq[E].T @ xs) + f64(b)[:, E:])
    xq = mxq(f64(xT)[:, idx], 0, "e4m3")
    y = by_expert(wq, xq)
    y = relu(y + np.repeat(f64(b)[:, :E], C, axis=1))
    return ys + f64(gate[0]) * y[:, unstriped(pos1)] + f64(gate[1]) * y[:, unstriped(pos2)]

@@ -1,0 +1,226 @@
+from contextlib import ExitStack
+
+import concourse.mybir as mybir
+
+K, T, E, C, N = 1024, 512, 4, 256, 384
+S = E * C
+P = 128
+K_PASS = 512
+PASSES = K // K_PASS
+N_TILES = N // P
+
+FLOPS = 2 * K * N * (S + T)
+
+F32 = mybir.dt.float32
+BF16 = mybir.dt.bfloat16
+U32 = mybir.dt.uint32
+U16 = mybir.dt.uint16
+U8 = mybir.dt.uint8
+FP8X4 = mybir.dt.float8_e4m3fn_x4
+ADD = mybir.AluOpType.add
+MAX = mybir.AluOpType.max
+MULT = mybir.AluOpType.mult
+RELU = mybir.ActivationFunctionType.Relu
+
+W_PLAN = [
+    [(0, 0, 384, "s"), (1, 0, 384, "s")],
+    [(0, 0, 384, "s"), (1, 0, 384, "s")],
+    [(0, 0, 384, "s"), (1, 0, 256, "s"), (1, 256, 128, "v")],
+    [(0, 0, 256, "s"), (0, 256, 128, "v"), (1, 0, 128, "s"), (1, 128, 256, "v")],
+    [(0, 0, 128, "s"), (0, 128, 128, "s"), (0, 256, 128, "s"), (1, 0, 128, "s"), (1, 128, 128, "s"), (1, 256, 128, "s")],
+]
+
+
+def tile_moe_shr_lin_relu_kernel(tc, xT, w, b, gate, offs, pos1, pos2, out):
+    nc = tc.nc
+    with ExitStack() as ctx:
+        keep = ctx.enter_context(tc.tile_pool(name="keep", bufs=1))
+        psum = ctx.enter_context(tc.psum_pool(name="psum", bufs=8))
+
+        x_raw = [keep.tile([P, 4, T], F32, name=f"x_raw{c}") for c in range(PASSES)]
+
+        def load_x(c, u):
+            rows = xT[c * K_PASS : (c + 1) * K_PASS, :].rearrange("(p j) t -> p j t", j=4)
+            nc.sync.dma_start(out=x_raw[c][:, 2 * u : 2 * u + 2, :], in_=rows[:, 2 * u : 2 * u + 2, :])
+
+        load_x(0, 1)
+        offs_t = keep.tile([P, S // 16], U16, name="offs_t")
+        nc.sync.dma_start(offs_t[:], offs)
+        load_x(0, 0)
+        load_x(1, 1)
+        load_x(1, 0)
+        bias = keep.tile([P, N_TILES, E + 1], F32, name="bias")
+        nc.scalar.dma_start(out=bias[:], in_=b.rearrange("(n p) e -> p n e", p=P))
+
+        w_raw = {}
+
+        def load_w(e, c):
+            tile = keep.tile([P, 4, N], F32, name=f"w_raw{e}_{c}")
+            nc.sync.dma_start(out=tile[:], in_=w[e, c * K_PASS : (c + 1) * K_PASS, :].rearrange("(p j) n -> p j n", j=4))
+            w_raw[e, c] = tile
+
+        load_w(0, 0)
+        load_w(0, 1)
+        pos1_t = keep.tile([P, T // 16], U16, name="pos1_t")
+        nc.sync.dma_start(pos1_t[:], pos1)
+        pos2_t = keep.tile([P, T // 16], U16, name="pos2_t")
+        nc.sync.dma_start(pos2_t[:], pos2)
+        for e in range(1, E):
+            for c in range(PASSES):
+                load_w(e, c)
+        gates = []
+
+        def load_gate(n):
+            tile = keep.tile([P, 2, T], F32, name=f"gate{n}")
+            nc.sync.dma_start(out=tile[:], in_=gate[:, n * P : (n + 1) * P, :].rearrange("r p t -> p r t"))
+            gates.append(tile)
+
+        load_gate(0)
+        load_w(E, 0)
+        load_gate(1)
+        load_w(E, 1)
+        load_gate(2)
+
+        neg_bias = keep.tile([P, N_TILES], F32, name="neg_bias")
+        nc.vector.tensor_scalar_mul(neg_bias[:], bias[:, :, E], -1.0)
+
+        planes = keep.tile([P, 4 * T * 2], BF16, name="planes")
+        words = planes[:].bitcast(U32)
+
+        def plane_at(c, u):
+            return (2 * (1 - c) + u) * T
+
+        def cast_plane(copy, c, u):
+            a = plane_at(c, u) * 2
+            copy(
+                out=planes[:, a : a + 2 * T].rearrange("p (g i e) -> p g e i", e=2, i=4),
+                in_=x_raw[c][:, 2 * u : 2 * u + 2, :].rearrange("p e (g i) -> p g e i", i=4),
+            )
+
+        cast_plane(nc.vector.tensor_copy, 0, 1)
+        cast_plane(nc.scalar.copy, 0, 0)
+        cast_plane(nc.scalar.copy, 1, 1)
+        cast_plane(nc.scalar.copy, 1, 0)
+
+        xg = [keep.tile([P, S * 4], BF16, name=f"xg{c}", align_bytes=64) for c in range(PASSES)]
+
+        def gather_plane(c, u, pieces, window):
+            a = plane_at(c, u)
+            dst = xg[c][:].bitcast(U32).rearrange("p (s v) -> p s v", v=2)
+            s0 = 0
+            for n in pieces:
+                nc.vector.tensor_copy(
+                    out=dst[:, s0 : s0 + n, u],
+                    in_=words[:, a : a + window].indirect(offs_t[:, s0 // 16 : (s0 + n) // 16]),
+                )
+                s0 += n
+
+        x_codes = [keep.tile([P, S], U32, name=f"x_codes{c}", align_bytes=64) for c in range(PASSES)]
+        x_scales = [keep.tile([P, S], U8, name=f"x_scales{c}", align_bytes=64) for c in range(PASSES)]
+
+        def quantize(codes, scales, src, a, n):
+            nc.vector.quantize_mx(
+                out=codes[:, a : a + n].bitcast(FP8X4), scales=scales[:, a : a + n], in_=src[:, 4 * a : 4 * (a + n)]
+            )
+
+        xs = [keep.tile([P, T * 4], BF16, name=f"xs{c}", align_bytes=64) for c in range(PASSES)]
+
+        for c in range(PASSES):
+            nc.gpsimd.tensor_scalar(
+                out=xs[c][:].rearrange("p (g i j) -> p g j i", i=4, j=4),
+                in0=x_raw[c][:].rearrange("p j (g i) -> p g j i", i=4),
+                scalar1=1.0, scalar2=0.0, op0=MULT, op1=ADD,
+            )
+        gather_plane(0, 1, (384, 384, 256), T)
+        gather_plane(0, 0, (512, 512), 2 * T)
+        gather_plane(1, 1, (1024,), 3 * T)
+        quantize(x_codes[0], x_scales[0], xg[0], 0, 512)
+        quantize(x_codes[0], x_scales[0], xg[0], 512, 512)
+        gather_plane(1, 0, (1024,), 4 * T)
+        xs_codes = [keep.tile([P, T], U32, name=f"xs_codes{c}", align_bytes=64) for c in range(PASSES)]
+        xs_scales = [keep.tile([P, T], U8, name=f"xs_scales{c}", align_bytes=64) for c in range(PASSES)]
+        quantize(x_codes[1], x_scales[1], xg[1], 0, 512)
+        quantize(x_codes[1], x_scales[1], xg[1], 512, 512)
+
+        w_grp, w_codes, w_scales = {}, {}, {}
+
+        def group_w(e):
+            tile = keep.tile([P, PASSES * N * 4], BF16, name=f"w_grp{e}", align_bytes=64)
+            w_grp[e] = tile
+
+            def piece(c, a, n):
+                col = c * N + a
+                return (
+                    tile[:, 4 * col : 4 * (col + n)].rearrange("p (g i j) -> p g j i", i=4, j=4),
+                    w_raw[e, c][:, :, a : a + n].rearrange("p j (g i) -> p g j i", i=4),
+                )
+
+            for c, a, n, engine in W_PLAN[e]:
+                o, i = piece(c, a, n)
+                if engine == "s":
+                    nc.scalar.copy(out=o, in_=i)
+                elif engine == "v":
+                    nc.vector.tensor_copy(out=o, in_=i)
+                else:
+                    nc.gpsimd.tensor_scalar(out=o, in0=i, scalar1=1.0, scalar2=0.0, op0=MULT, op1=ADD)
+
+        def quantize_w(e):
+            w_codes[e] = keep.tile([P, PASSES * N], U32, name=f"w_codes{e}", align_bytes=64)
+            w_scales[e] = keep.tile([P, PASSES * N], U8, name=f"w_scales{e}", align_bytes=64)
+            quantize(w_codes[e], w_scales[e], w_grp[e], 0, 512)
+            quantize(w_codes[e], w_scales[e], w_grp[e], 512, 256)
+
+        def product(acc, e, n, codes, scales, s0, width):
+            for c in range(PASSES):
+                cols = slice(c * N + n * P, c * N + (n + 1) * P)
+                nc.tensor.matmul_mx(
+                    out=acc[:],
+                    lhsT=w_codes[e][:, cols].bitcast(FP8X4),
+                    lhsT_scale=w_scales[e][:, cols],
+                    rhs=codes[c][:, s0 : s0 + width].bitcast(FP8X4),
+                    rhs_scale=scales[c][:, s0 : s0 + width],
+                    start=(c == 0),
+                    stop=(c == PASSES - 1),
+                )
+
+        y = [keep.tile([P, S], F32, name=f"y{n}") for n in range(N_TILES)]
+        for e in range(E):
+            group_w(e)
+        for e in range(E):
+            quantize_w(e)
+            for n in range(N_TILES):
+                acc = psum.tile([P, C], F32, name="acc")
+                product(acc, e, n, x_codes, x_scales, e * C, C)
+                nc.scalar.activation(
+                    out=y[n][:, e * C : (e + 1) * C], in_=acc[:], func=RELU, bias=bias[:, n, e : e + 1], scale=1.0
+                )
+
+        for c in range(PASSES):
+            quantize(xs_codes[c], xs_scales[c], xs[c], 0, T)
+
+        mixed = []
+
+        def combine(n):
+            t1 = keep.tile([P, T], F32, name=f"t1_{n}")
+            nc.vector.tensor_tensor(out=t1[:], in0=y[n][:].indirect(pos1_t[:]), in1=gates[n][:, 0, :], op=MULT)
+            t2 = keep.tile([P, T], F32, name=f"t2_{n}")
+            nc.vector.tensor_tensor(out=t2[:], in0=y[n][:].indirect(pos2_t[:]), in1=gates[n][:, 1, :], op=MULT)
+            m = keep.tile([P, T], F32, name=f"m{n}")
+            nc.vector.scalar_tensor_tensor(
+                out=m[:], in0=t1[:], scalar=bias[:, n, E : E + 1], in1=t2[:], op0=ADD, op1=ADD
+            )
+            mixed.append(m)
+
+        group_w(E)
+        combine(0)
+        combine(1)
+        quantize_w(E)
+        combine(2)
+        for n in range(N_TILES):
+            acc = psum.tile([P, T], F32, name="acc")
+            product(acc, E, n, xs_codes, xs_scales, 0, T)
+            res = keep.tile([P, T], F32, name=f"res{n}")
+            nc.vector.scalar_tensor_tensor(
+                out=res[:], in0=acc[:], scalar=neg_bias[:, n : n + 1], in1=mixed[n][:], op0=MAX, op1=ADD
+            )
+            nc.sync.dma_start(out=out[n * P : (n + 1) * P, :], in_=res[:])

@@ -24,9 +24,9 @@ RELU = mybir.ActivationFunctionType.Relu
 
 W_PLAN = [
     [(0, 0, 384, "s"), (1, 0, 384, "s")],
-    [(0, 0, 384, "s"), (1, 0, 384, "s")],
-    [(0, 0, 384, "s"), (1, 0, 256, "s"), (1, 256, 128, "v")],
     [(0, 0, 256, "s"), (0, 256, 128, "v"), (1, 0, 128, "s"), (1, 128, 256, "v")],
+    [(0, 0, 384, "s"), (1, 0, 128, "s"), (1, 128, 256, "v")],
+    [(0, 0, 256, "s"), (0, 256, 128, "v"), (1, 0, 384, "v")],
     [(0, 0, 128, "s"), (0, 128, 128, "s"), (0, 256, 128, "s"), (1, 0, 128, "s"), (1, 128, 128, "s"), (1, 256, 128, "s")],
 ]
 
@@ -104,16 +104,23 @@ def tile_moe_shr_lin_relu_kernel(tc, xT, w, b, gate, offs, pos1, pos2, out):
 
         xg = [keep.tile([P, S * 4], BF16, name=f"xg{c}", align_bytes=64) for c in range(PASSES)]
 
+        picked = [keep.tile([P, 2 * S], U32, name=f"picked{c}") for c in range(PASSES)]
+
         def gather_plane(c, u, pieces, window):
             a = plane_at(c, u)
-            dst = xg[c][:].bitcast(U32).rearrange("p (s v) -> p s v", v=2)
             s0 = 0
             for n in pieces:
                 nc.vector.tensor_copy(
-                    out=dst[:, s0 : s0 + n, u],
+                    out=picked[c][:, u * S + s0 : u * S + s0 + n],
                     in_=words[:, a : a + window].indirect(offs_t[:, s0 // 16 : (s0 + n) // 16]),
                 )
                 s0 += n
+
+        def interleave(copy, c, a, n):
+            copy(
+                out=xg[c][:].bitcast(F32).rearrange("p (s u) -> p s u", u=2)[:, a : a + n, :],
+                in_=picked[c][:].bitcast(F32).rearrange("p (u s) -> p s u", u=2)[:, a : a + n, :],
+            )
 
         x_codes = [keep.tile([P, S], U32, name=f"x_codes{c}", align_bytes=64) for c in range(PASSES)]
         x_scales = [keep.tile([P, S], U8, name=f"x_scales{c}", align_bytes=64) for c in range(PASSES)]
@@ -125,18 +132,16 @@ def tile_moe_shr_lin_relu_kernel(tc, xT, w, b, gate, offs, pos1, pos2, out):
 
         xs = [keep.tile([P, T * 4], BF16, name=f"xs{c}", align_bytes=64) for c in range(PASSES)]
 
-        for c in range(PASSES):
-            nc.gpsimd.tensor_scalar(
-                out=xs[c][:].rearrange("p (g i j) -> p g j i", i=4, j=4),
-                in0=x_raw[c][:].rearrange("p j (g i) -> p g j i", i=4),
-                scalar1=1.0, scalar2=0.0, op0=MULT, op1=ADD,
-            )
         gather_plane(0, 1, (384, 384, 256), T)
         gather_plane(0, 0, (512, 512), 2 * T)
+        interleave(nc.scalar.copy, 0, 0, 512)
+        interleave(nc.scalar.copy, 0, 512, 512)
         gather_plane(1, 1, (1024,), 3 * T)
+        gather_plane(1, 0, (1024,), 4 * T)
         quantize(x_codes[0], x_scales[0], xg[0], 0, 512)
         quantize(x_codes[0], x_scales[0], xg[0], 512, 512)
-        gather_plane(1, 0, (1024,), 4 * T)
+        interleave(nc.scalar.copy, 1, 0, 512)
+        interleave(nc.vector.tensor_copy, 1, 512, 512)
         xs_codes = [keep.tile([P, T], U32, name=f"xs_codes{c}", align_bytes=64) for c in range(PASSES)]
         xs_scales = [keep.tile([P, T], U8, name=f"xs_scales{c}", align_bytes=64) for c in range(PASSES)]
         quantize(x_codes[1], x_scales[1], xg[1], 0, 512)
@@ -195,6 +200,12 @@ def tile_moe_shr_lin_relu_kernel(tc, xT, w, b, gate, offs, pos1, pos2, out):
                     out=y[n][:, e * C : (e + 1) * C], in_=acc[:], func=RELU, bias=bias[:, n, e : e + 1], scale=1.0
                 )
 
+        for c in range(PASSES):
+            a = plane_at(c, 0)
+            nc.vector.tensor_copy(
+                out=xs[c][:].bitcast(F32).rearrange("p (t u) -> p t u", u=2),
+                in_=planes[:].bitcast(F32)[:, a : a + 2 * T].rearrange("p (v t) -> p t v", v=2),
+            )
         for c in range(PASSES):
             quantize(xs_codes[c], xs_scales[c], xs[c], 0, T)
 

@@ -24,7 +24,7 @@ RELU = mybir.ActivationFunctionType.Relu
 
 W_PLAN = [
     [(0, 0, 384, "s"), (1, 0, 384, "s")],
-    [(0, 0, 256, "s"), (0, 256, 128, "v"), (1, 0, 128, "s"), (1, 128, 256, "v")],
+    [(0, 0, 384, "s"), (1, 0, 384, "s")],
     [(0, 0, 384, "s"), (1, 0, 128, "s"), (1, 128, 256, "v")],
     [(0, 0, 256, "s"), (0, 256, 128, "v"), (1, 0, 384, "v")],
     [(0, 0, 128, "s"), (0, 128, 128, "s"), (0, 256, 128, "s"), (1, 0, 128, "s"), (1, 128, 128, "s"), (1, 256, 128, "s")],
@@ -82,7 +82,7 @@ def tile_moe_shr_lin_relu_kernel(tc, xT, w, b, gate, offs, pos1, pos2, out):
         load_gate(2)
 
         neg_bias = keep.tile([P, N_TILES], F32, name="neg_bias")
-        nc.vector.tensor_scalar_mul(neg_bias[:], bias[:, :, E], -1.0)
+        nc.scalar.mul(neg_bias[:], bias[:, :, E], -1.0)
 
         planes = keep.tile([P, 4 * T * 2], BF16, name="planes")
         words = planes[:].bitcast(U32)
@@ -104,6 +104,13 @@ def tile_moe_shr_lin_relu_kernel(tc, xT, w, b, gate, offs, pos1, pos2, out):
 
         xg = [keep.tile([P, S * 4], BF16, name=f"xg{c}", align_bytes=64) for c in range(PASSES)]
 
+        xs = [keep.tile([P, T * 4], BF16, name=f"xs{c}", align_bytes=64) for c in range(PASSES)]
+        for c in range(PASSES):
+            nc.gpsimd.tensor_scalar(
+                out=xs[c][:].rearrange("p (g i j) -> p g j i", i=4, j=4),
+                in0=x_raw[c][:].rearrange("p j (g i) -> p g j i", i=4),
+                scalar1=1.0, scalar2=0.0, op0=MULT, op1=ADD,
+            )
         picked = [keep.tile([P, 2 * S], U32, name=f"picked{c}") for c in range(PASSES)]
 
         def gather_plane(c, u, pieces, window):
@@ -130,7 +137,6 @@ def tile_moe_shr_lin_relu_kernel(tc, xT, w, b, gate, offs, pos1, pos2, out):
                 out=codes[:, a : a + n].bitcast(FP8X4), scales=scales[:, a : a + n], in_=src[:, 4 * a : 4 * (a + n)]
             )
 
-        xs = [keep.tile([P, T * 4], BF16, name=f"xs{c}", align_bytes=64) for c in range(PASSES)]
 
         gather_plane(0, 1, (384, 384, 256), T)
         gather_plane(0, 0, (512, 512), 2 * T)
@@ -138,14 +144,12 @@ def tile_moe_shr_lin_relu_kernel(tc, xT, w, b, gate, offs, pos1, pos2, out):
         interleave(nc.scalar.copy, 0, 512, 512)
         gather_plane(1, 1, (1024,), 3 * T)
         gather_plane(1, 0, (1024,), 4 * T)
-        quantize(x_codes[0], x_scales[0], xg[0], 0, 512)
-        quantize(x_codes[0], x_scales[0], xg[0], 512, 512)
+        quantize(x_codes[0], x_scales[0], xg[0], 0, S)
         interleave(nc.scalar.copy, 1, 0, 512)
         interleave(nc.vector.tensor_copy, 1, 512, 512)
         xs_codes = [keep.tile([P, T], U32, name=f"xs_codes{c}", align_bytes=64) for c in range(PASSES)]
         xs_scales = [keep.tile([P, T], U8, name=f"xs_scales{c}", align_bytes=64) for c in range(PASSES)]
-        quantize(x_codes[1], x_scales[1], xg[1], 0, 512)
-        quantize(x_codes[1], x_scales[1], xg[1], 512, 512)
+        quantize(x_codes[1], x_scales[1], xg[1], 0, S)
 
         w_grp, w_codes, w_scales = {}, {}, {}
 
@@ -201,12 +205,6 @@ def tile_moe_shr_lin_relu_kernel(tc, xT, w, b, gate, offs, pos1, pos2, out):
                 )
 
         for c in range(PASSES):
-            a = plane_at(c, 0)
-            nc.vector.tensor_copy(
-                out=xs[c][:].bitcast(F32).rearrange("p (t u) -> p t u", u=2),
-                in_=planes[:].bitcast(F32)[:, a : a + 2 * T].rearrange("p (v t) -> p t v", v=2),
-            )
-        for c in range(PASSES):
             quantize(xs_codes[c], xs_scales[c], xs[c], 0, T)
 
         mixed = []
@@ -223,9 +221,9 @@ def tile_moe_shr_lin_relu_kernel(tc, xT, w, b, gate, offs, pos1, pos2, out):
             mixed.append(m)
 
         group_w(E)
+        quantize_w(E)
         combine(0)
         combine(1)
-        quantize_w(E)
         combine(2)
         for n in range(N_TILES):
             acc = psum.tile([P, T], F32, name="acc")

@@ -22,10 +22,11 @@ MAX = mybir.AluOpType.max
 MULT = mybir.AluOpType.mult
 RELU = mybir.ActivationFunctionType.Relu
 
+SLOT_OF = {(0, 0): "slot_x0", (0, 1): "slot_x1", (2, 1): "slot_y0", (3, 0): "slot_y1", (3, 1): "slot_y2"}
 W_PLAN = [
     [(0, 0, 384, "s"), (1, 0, 384, "s")],
     [(0, 0, 384, "s"), (1, 0, 384, "s")],
-    [(0, 0, 384, "s"), (1, 0, 128, "s"), (1, 128, 256, "v")],
+    [(0, 0, 384, "v"), (1, 0, 384, "s")],
     [(0, 0, 256, "s"), (0, 256, 128, "v"), (1, 0, 384, "v")],
     [(0, 0, 128, "s"), (0, 128, 128, "s"), (0, 256, 128, "s"), (1, 0, 128, "s"), (1, 128, 128, "s"), (1, 256, 128, "s")],
 ]
@@ -35,46 +36,50 @@ def tile_moe_shr_lin_relu_kernel(tc, xT, w, b, gate, offs, pos1, pos2, out):
     nc = tc.nc
     with ExitStack() as ctx:
         keep = ctx.enter_context(tc.tile_pool(name="keep", bufs=1))
+        swap = ctx.enter_context(tc.tile_pool(name="swap", bufs=1))
         psum = ctx.enter_context(tc.psum_pool(name="psum", bufs=8))
 
         x_raw = [keep.tile([P, 4, T], F32, name=f"x_raw{c}") for c in range(PASSES)]
+        lists = {}
 
-        def load_x(c, u):
+        def load_list(name, source):
+            lists[name] = keep.tile([P, source.shape[1]], U16, name=name)
+            nc.sync.dma_start(lists[name][:], source)
+
+        def load_x(c, u, t0=0, t1=T):
             rows = xT[c * K_PASS : (c + 1) * K_PASS, :].rearrange("(p j) t -> p j t", j=4)
-            nc.sync.dma_start(out=x_raw[c][:, 2 * u : 2 * u + 2, :], in_=rows[:, 2 * u : 2 * u + 2, :])
+            nc.sync.dma_start(out=x_raw[c][:, 2 * u : 2 * u + 2, t0:t1], in_=rows[:, 2 * u : 2 * u + 2, t0:t1])
 
-        load_x(0, 1)
-        offs_t = keep.tile([P, S // 16], U16, name="offs_t")
-        nc.sync.dma_start(offs_t[:], offs)
+        load_x(0, 1, 0, T // 2)
+        load_list("offs", offs)
+        load_x(0, 1, T // 2, T)
         load_x(0, 0)
         load_x(1, 1)
         load_x(1, 0)
         bias = keep.tile([P, N_TILES, E + 1], F32, name="bias")
         nc.scalar.dma_start(out=bias[:], in_=b.rearrange("(n p) e -> p n e", p=P))
-
-        w_raw = {}
+        w_raw, gates = {}, []
 
         def load_w(e, c):
-            tile = keep.tile([P, 4, N], F32, name=f"w_raw{e}_{c}")
+            if (e, c) in SLOT_OF:
+                tile = swap.tile([P, 4, N], F32, name=f"w_raw{e}_{c}", tag=SLOT_OF[e, c], align_bytes=64)
+            else:
+                tile = keep.tile([P, 4, N], F32, name=f"w_raw{e}_{c}")
             nc.sync.dma_start(out=tile[:], in_=w[e, c * K_PASS : (c + 1) * K_PASS, :].rearrange("(p j) n -> p j n", j=4))
             w_raw[e, c] = tile
-
-        load_w(0, 0)
-        load_w(0, 1)
-        pos1_t = keep.tile([P, T // 16], U16, name="pos1_t")
-        nc.sync.dma_start(pos1_t[:], pos1)
-        pos2_t = keep.tile([P, T // 16], U16, name="pos2_t")
-        nc.sync.dma_start(pos2_t[:], pos2)
-        for e in range(1, E):
-            for c in range(PASSES):
-                load_w(e, c)
-        gates = []
 
         def load_gate(n):
             tile = keep.tile([P, 2, T], F32, name=f"gate{n}")
             nc.sync.dma_start(out=tile[:], in_=gate[:, n * P : (n + 1) * P, :].rearrange("r p t -> p r t"))
             gates.append(tile)
 
+        load_w(0, 0)
+        load_w(0, 1)
+        load_list("pos1", pos1)
+        load_list("pos2", pos2)
+        for e in range(1, E):
+            for c in range(PASSES):
+                load_w(e, c)
         load_gate(0)
         load_w(E, 0)
         load_gate(1)
@@ -84,34 +89,37 @@ def tile_moe_shr_lin_relu_kernel(tc, xT, w, b, gate, offs, pos1, pos2, out):
         neg_bias = keep.tile([P, N_TILES], F32, name="neg_bias")
         nc.scalar.mul(neg_bias[:], bias[:, :, E], -1.0)
 
+        def gpsimd_copy(out, in_):
+            nc.gpsimd.tensor_scalar(out=out, in0=in_, scalar1=1.0, scalar2=0.0, op0=MULT, op1=ADD)
+
         planes = keep.tile([P, 4 * T * 2], BF16, name="planes")
         words = planes[:].bitcast(U32)
 
         def plane_at(c, u):
             return (2 * (1 - c) + u) * T
 
-        def cast_plane(copy, c, u):
-            a = plane_at(c, u) * 2
+        def cast_plane(copy, c, u, t0=0, t1=T):
+            a = plane_at(c, u)
             copy(
-                out=planes[:, a : a + 2 * T].rearrange("p (g i e) -> p g e i", e=2, i=4),
-                in_=x_raw[c][:, 2 * u : 2 * u + 2, :].rearrange("p e (g i) -> p g e i", i=4),
+                out=planes[:, 2 * (a + t0) : 2 * (a + t1)].rearrange("p (g i e) -> p g e i", e=2, i=4),
+                in_=x_raw[c][:, 2 * u : 2 * u + 2, t0:t1].rearrange("p e (g i) -> p g e i", i=4),
             )
 
-        cast_plane(nc.vector.tensor_copy, 0, 1)
+        cast_plane(nc.vector.tensor_copy, 0, 1, 0, T // 2)
+        cast_plane(nc.vector.tensor_copy, 0, 1, T // 2, T)
         cast_plane(nc.scalar.copy, 0, 0)
         cast_plane(nc.scalar.copy, 1, 1)
         cast_plane(nc.scalar.copy, 1, 0)
 
-        xg = [keep.tile([P, S * 4], BF16, name=f"xg{c}", align_bytes=64) for c in range(PASSES)]
-
-        xs = [keep.tile([P, T * 4], BF16, name=f"xs{c}", align_bytes=64) for c in range(PASSES)]
+        xs = keep.tile([P, PASSES * T * 4], BF16, name="xs", align_bytes=64)
         for c in range(PASSES):
-            nc.gpsimd.tensor_scalar(
-                out=xs[c][:].rearrange("p (g i j) -> p g j i", i=4, j=4),
-                in0=x_raw[c][:].rearrange("p j (g i) -> p g j i", i=4),
-                scalar1=1.0, scalar2=0.0, op0=MULT, op1=ADD,
+            gpsimd_copy(
+                out=xs[:, 4 * c * T : 4 * (c + 1) * T].rearrange("p (g i j) -> p g j i", i=4, j=4),
+                in_=x_raw[c][:].rearrange("p j (g i) -> p g j i", i=4),
             )
+
         picked = [keep.tile([P, 2 * S], U32, name=f"picked{c}") for c in range(PASSES)]
+        xg = [swap.tile([P, S * 4], BF16, name=f"xg{c}", tag=f"slot_x{c}", align_bytes=64) for c in range(PASSES)]
 
         def gather_plane(c, u, pieces, window):
             a = plane_at(c, u)
@@ -119,7 +127,7 @@ def tile_moe_shr_lin_relu_kernel(tc, xT, w, b, gate, offs, pos1, pos2, out):
             for n in pieces:
                 nc.vector.tensor_copy(
                     out=picked[c][:, u * S + s0 : u * S + s0 + n],
-                    in_=words[:, a : a + window].indirect(offs_t[:, s0 // 16 : (s0 + n) // 16]),
+                    in_=words[:, a : a + window].indirect(lists["offs"][:, s0 // 16 : (s0 + n) // 16]),
                 )
                 s0 += n
 
@@ -129,49 +137,35 @@ def tile_moe_shr_lin_relu_kernel(tc, xT, w, b, gate, offs, pos1, pos2, out):
                 in_=picked[c][:].bitcast(F32).rearrange("p (u s) -> p s u", u=2)[:, a : a + n, :],
             )
 
-        x_codes = [keep.tile([P, S], U32, name=f"x_codes{c}", align_bytes=64) for c in range(PASSES)]
-        x_scales = [keep.tile([P, S], U8, name=f"x_scales{c}", align_bytes=64) for c in range(PASSES)]
-
         def quantize(codes, scales, src, a, n):
             nc.vector.quantize_mx(
                 out=codes[:, a : a + n].bitcast(FP8X4), scales=scales[:, a : a + n], in_=src[:, 4 * a : 4 * (a + n)]
             )
 
-
+        x_codes = [keep.tile([P, S], U32, name=f"x_codes{c}", align_bytes=64) for c in range(PASSES)]
+        x_scales = [keep.tile([P, S], U8, name=f"x_scales{c}", align_bytes=64) for c in range(PASSES)]
         gather_plane(0, 1, (384, 384, 256), T)
         gather_plane(0, 0, (512, 512), 2 * T)
-        interleave(nc.scalar.copy, 0, 0, 512)
-        interleave(nc.scalar.copy, 0, 512, 512)
+        interleave(nc.scalar.copy, 0, 0, 768)
+        interleave(nc.vector.tensor_copy, 0, 768, 256)
         gather_plane(1, 1, (1024,), 3 * T)
         gather_plane(1, 0, (1024,), 4 * T)
         quantize(x_codes[0], x_scales[0], xg[0], 0, S)
-        interleave(nc.scalar.copy, 1, 0, 512)
-        interleave(nc.vector.tensor_copy, 1, 512, 512)
-        xs_codes = [keep.tile([P, T], U32, name=f"xs_codes{c}", align_bytes=64) for c in range(PASSES)]
-        xs_scales = [keep.tile([P, T], U8, name=f"xs_scales{c}", align_bytes=64) for c in range(PASSES)]
+        interleave(nc.vector.tensor_copy, 1, 0, 1024)
         quantize(x_codes[1], x_scales[1], xg[1], 0, S)
 
         w_grp, w_codes, w_scales = {}, {}, {}
+        copies = {"s": nc.scalar.copy, "v": nc.vector.tensor_copy, "g": gpsimd_copy}
 
         def group_w(e):
-            tile = keep.tile([P, PASSES * N * 4], BF16, name=f"w_grp{e}", align_bytes=64)
-            w_grp[e] = tile
-
-            def piece(c, a, n):
-                col = c * N + a
-                return (
-                    tile[:, 4 * col : 4 * (col + n)].rearrange("p (g i j) -> p g j i", i=4, j=4),
-                    w_raw[e, c][:, :, a : a + n].rearrange("p j (g i) -> p g j i", i=4),
-                )
-
+            pool, tag = (swap, "slot_grp") if e == 3 else (keep, f"w_grp{e}")
+            w_grp[e] = pool.tile([P, PASSES * N * 4], BF16, name=f"w_grp{e}", tag=tag, align_bytes=64)
             for c, a, n, engine in W_PLAN[e]:
-                o, i = piece(c, a, n)
-                if engine == "s":
-                    nc.scalar.copy(out=o, in_=i)
-                elif engine == "v":
-                    nc.vector.tensor_copy(out=o, in_=i)
-                else:
-                    nc.gpsimd.tensor_scalar(out=o, in0=i, scalar1=1.0, scalar2=0.0, op0=MULT, op1=ADD)
+                col = c * N + a
+                copies[engine](
+                    out=w_grp[e][:, 4 * col : 4 * (col + n)].rearrange("p (g i j) -> p g j i", i=4, j=4),
+                    in_=w_raw[e, c][:, :, a : a + n].rearrange("p j (g i) -> p g j i", i=4),
+                )
 
         def quantize_w(e):
             w_codes[e] = keep.tile([P, PASSES * N], U32, name=f"w_codes{e}", align_bytes=64)
@@ -179,55 +173,56 @@ def tile_moe_shr_lin_relu_kernel(tc, xT, w, b, gate, offs, pos1, pos2, out):
             quantize(w_codes[e], w_scales[e], w_grp[e], 0, 512)
             quantize(w_codes[e], w_scales[e], w_grp[e], 512, 256)
 
-        def product(acc, e, n, codes, scales, s0, width):
+        def product(acc, e, n, moving):
             for c in range(PASSES):
                 cols = slice(c * N + n * P, c * N + (n + 1) * P)
+                codes, scales = moving[c]
                 nc.tensor.matmul_mx(
                     out=acc[:],
                     lhsT=w_codes[e][:, cols].bitcast(FP8X4),
                     lhsT_scale=w_scales[e][:, cols],
-                    rhs=codes[c][:, s0 : s0 + width].bitcast(FP8X4),
-                    rhs_scale=scales[c][:, s0 : s0 + width],
+                    rhs=codes.bitcast(FP8X4),
+                    rhs_scale=scales,
                     start=(c == 0),
                     stop=(c == PASSES - 1),
                 )
 
-        y = [keep.tile([P, S], F32, name=f"y{n}") for n in range(N_TILES)]
         for e in range(E):
             group_w(e)
         for e in range(E):
             quantize_w(e)
-            for n in range(N_TILES):
+        xs_codes = swap.tile([P, PASSES * T], U32, name="xs_codes", tag="slot_grp", align_bytes=64)
+        xs_scales = keep.tile([P, PASSES * T], U8, name="xs_scales", align_bytes=64)
+        quantize(xs_codes, xs_scales, xs, 0, 2 * T)
+        y = []
+        for n in range(N_TILES):
+            y.append(swap.tile([P, S], F32, name=f"y{n}", tag=f"slot_y{n}", align_bytes=64))
+            for e in range(E):
+                slots = slice(e * C, (e + 1) * C)
                 acc = psum.tile([P, C], F32, name="acc")
-                product(acc, e, n, x_codes, x_scales, e * C, C)
-                nc.scalar.activation(
-                    out=y[n][:, e * C : (e + 1) * C], in_=acc[:], func=RELU, bias=bias[:, n, e : e + 1], scale=1.0
-                )
-
-        for c in range(PASSES):
-            quantize(xs_codes[c], xs_scales[c], xs[c], 0, T)
+                product(acc, e, n, [(x_codes[c][:, slots], x_scales[c][:, slots]) for c in range(PASSES)])
+                nc.scalar.activation(out=y[n][:, slots], in_=acc[:], func=RELU, bias=bias[:, n, e : e + 1], scale=1.0)
 
         mixed = []
 
         def combine(n):
             t1 = keep.tile([P, T], F32, name=f"t1_{n}")
-            nc.vector.tensor_tensor(out=t1[:], in0=y[n][:].indirect(pos1_t[:]), in1=gates[n][:, 0, :], op=MULT)
+            nc.vector.tensor_tensor(out=t1[:], in0=y[n][:].indirect(lists["pos1"][:]), in1=gates[n][:, 0, :], op=MULT)
             t2 = keep.tile([P, T], F32, name=f"t2_{n}")
-            nc.vector.tensor_tensor(out=t2[:], in0=y[n][:].indirect(pos2_t[:]), in1=gates[n][:, 1, :], op=MULT)
-            m = keep.tile([P, T], F32, name=f"m{n}")
+            nc.vector.tensor_tensor(out=t2[:], in0=y[n][:].indirect(lists["pos2"][:]), in1=gates[n][:, 1, :], op=MULT)
+            mixed.append(keep.tile([P, T], F32, name=f"mixed{n}"))
             nc.vector.scalar_tensor_tensor(
-                out=m[:], in0=t1[:], scalar=bias[:, n, E : E + 1], in1=t2[:], op0=ADD, op1=ADD
+                out=mixed[n][:], in0=t1[:], scalar=bias[:, n, E : E + 1], in1=t2[:], op0=ADD, op1=ADD
             )
-            mixed.append(m)
 
+        combine(0)
         group_w(E)
         quantize_w(E)
-        combine(0)
         combine(1)
         combine(2)
         for n in range(N_TILES):
             acc = psum.tile([P, T], F32, name="acc")
-            product(acc, E, n, xs_codes, xs_scales, 0, T)
+            product(acc, E, n, [(xs_codes[:, c * T : (c + 1) * T], xs_scales[:, c * T : (c + 1) * T]) for c in range(PASSES)])
             res = keep.tile([P, T], F32, name=f"res{n}")
             nc.vector.scalar_tensor_tensor(
                 out=res[:], in0=acc[:], scalar=neg_bias[:, n : n + 1], in1=mixed[n][:], op0=MAX, op1=ADD

from contextlib import ExitStack

import concourse.mybir as mybir

K, T, E, C, N = 1024, 512, 4, 256, 384
S = E * C
P = 128
K_PASS = 512
PASSES = K // K_PASS
N_TILES = N // P

FLOPS = 2 * K * N * (S + T)

F32 = mybir.dt.float32
BF16 = mybir.dt.bfloat16
U32 = mybir.dt.uint32
U16 = mybir.dt.uint16
U8 = mybir.dt.uint8
FP8X4 = mybir.dt.float8_e4m3fn_x4
ADD = mybir.AluOpType.add
MAX = mybir.AluOpType.max
MULT = mybir.AluOpType.mult
RELU = mybir.ActivationFunctionType.Relu

SLOT_OF = {(0, 0): "slot_x0", (0, 1): "slot_x1", (2, 1): "slot_y0", (3, 0): "slot_y1", (3, 1): "slot_y2"}
W_PLAN = [
    [(0, 0, 384, "s"), (1, 0, 384, "s")],
    [(0, 0, 384, "s"), (1, 0, 384, "s")],
    [(0, 0, 384, "v"), (1, 0, 384, "s")],
    [(0, 0, 256, "s"), (0, 256, 128, "v"), (1, 0, 384, "v")],
    [(0, 0, 128, "s"), (0, 128, 128, "s"), (0, 256, 128, "s"), (1, 0, 128, "s"), (1, 128, 128, "s"), (1, 256, 128, "s")],
]


def tile_moe_shr_lin_relu_kernel(tc, xT, w, b, gate, offs, pos1, pos2, out):
    nc = tc.nc
    with ExitStack() as ctx:
        keep = ctx.enter_context(tc.tile_pool(name="keep", bufs=1))
        swap = ctx.enter_context(tc.tile_pool(name="swap", bufs=1))
        psum = ctx.enter_context(tc.psum_pool(name="psum", bufs=8))

        x_raw = [keep.tile([P, 4, T], F32, name=f"x_raw{c}") for c in range(PASSES)]
        lists = {}

        def load_list(name, source):
            lists[name] = keep.tile([P, source.shape[1]], U16, name=name)
            nc.sync.dma_start(lists[name][:], source)

        def load_x(c, u, t0=0, t1=T):
            rows = xT[c * K_PASS : (c + 1) * K_PASS, :].rearrange("(p j) t -> p j t", j=4)
            nc.sync.dma_start(out=x_raw[c][:, 2 * u : 2 * u + 2, t0:t1], in_=rows[:, 2 * u : 2 * u + 2, t0:t1])

        load_x(0, 1, 0, T // 2)
        load_list("offs", offs)
        load_x(0, 1, T // 2, T)
        load_x(0, 0)
        load_x(1, 1)
        load_x(1, 0)
        bias = keep.tile([P, N_TILES, E + 1], F32, name="bias")
        nc.scalar.dma_start(out=bias[:], in_=b.rearrange("(n p) e -> p n e", p=P))
        w_raw, gates = {}, []

        def load_w(e, c):
            if (e, c) in SLOT_OF:
                tile = swap.tile([P, 4, N], F32, name=f"w_raw{e}_{c}", tag=SLOT_OF[e, c], align_bytes=64)
            else:
                tile = keep.tile([P, 4, N], F32, name=f"w_raw{e}_{c}")
            nc.sync.dma_start(out=tile[:], in_=w[e, c * K_PASS : (c + 1) * K_PASS, :].rearrange("(p j) n -> p j n", j=4))
            w_raw[e, c] = tile

        def load_gate(n):
            tile = keep.tile([P, 2, T], F32, name=f"gate{n}")
            nc.sync.dma_start(out=tile[:], in_=gate[:, n * P : (n + 1) * P, :].rearrange("r p t -> p r t"))
            gates.append(tile)

        load_w(0, 0)
        load_w(0, 1)
        load_list("pos1", pos1)
        load_list("pos2", pos2)
        for e in range(1, E):
            for c in range(PASSES):
                load_w(e, c)
        load_gate(0)
        load_w(E, 0)
        load_gate(1)
        load_w(E, 1)
        load_gate(2)

        neg_bias = keep.tile([P, N_TILES], F32, name="neg_bias")
        nc.scalar.mul(neg_bias[:], bias[:, :, E], -1.0)

        def gpsimd_copy(out, in_):
            nc.gpsimd.tensor_scalar(out=out, in0=in_, scalar1=1.0, scalar2=0.0, op0=MULT, op1=ADD)

        planes = keep.tile([P, 4 * T * 2], BF16, name="planes")
        words = planes[:].bitcast(U32)

        def plane_at(c, u):
            return (2 * (1 - c) + u) * T

        def cast_plane(copy, c, u, t0=0, t1=T):
            a = plane_at(c, u)
            copy(
                out=planes[:, 2 * (a + t0) : 2 * (a + t1)].rearrange("p (g i e) -> p g e i", e=2, i=4),
                in_=x_raw[c][:, 2 * u : 2 * u + 2, t0:t1].rearrange("p e (g i) -> p g e i", i=4),
            )

        cast_plane(nc.vector.tensor_copy, 0, 1, 0, T // 2)
        cast_plane(nc.vector.tensor_copy, 0, 1, T // 2, T)
        cast_plane(nc.scalar.copy, 0, 0)
        cast_plane(nc.scalar.copy, 1, 1)
        cast_plane(nc.scalar.copy, 1, 0)

        xs = keep.tile([P, PASSES * T * 4], BF16, name="xs", align_bytes=64)
        for c in range(PASSES):
            gpsimd_copy(
                out=xs[:, 4 * c * T : 4 * (c + 1) * T].rearrange("p (g i j) -> p g j i", i=4, j=4),
                in_=x_raw[c][:].rearrange("p j (g i) -> p g j i", i=4),
            )

        picked = [keep.tile([P, 2 * S], U32, name=f"picked{c}") for c in range(PASSES)]
        xg = [swap.tile([P, S * 4], BF16, name=f"xg{c}", tag=f"slot_x{c}", align_bytes=64) for c in range(PASSES)]

        def gather_plane(c, u, pieces, window):
            a = plane_at(c, u)
            s0 = 0
            for n in pieces:
                nc.vector.tensor_copy(
                    out=picked[c][:, u * S + s0 : u * S + s0 + n],
                    in_=words[:, a : a + window].indirect(lists["offs"][:, s0 // 16 : (s0 + n) // 16]),
                )
                s0 += n

        def interleave(copy, c, a, n):
            copy(
                out=xg[c][:].bitcast(F32).rearrange("p (s u) -> p s u", u=2)[:, a : a + n, :],
                in_=picked[c][:].bitcast(F32).rearrange("p (u s) -> p s u", u=2)[:, a : a + n, :],
            )

        def quantize(codes, scales, src, a, n):
            nc.vector.quantize_mx(
                out=codes[:, a : a + n].bitcast(FP8X4), scales=scales[:, a : a + n], in_=src[:, 4 * a : 4 * (a + n)]
            )

        x_codes = [keep.tile([P, S], U32, name=f"x_codes{c}", align_bytes=64) for c in range(PASSES)]
        x_scales = [keep.tile([P, S], U8, name=f"x_scales{c}", align_bytes=64) for c in range(PASSES)]
        gather_plane(0, 1, (384, 384, 256), T)
        gather_plane(0, 0, (512, 512), 2 * T)
        interleave(nc.scalar.copy, 0, 0, 768)
        interleave(nc.vector.tensor_copy, 0, 768, 256)
        gather_plane(1, 1, (1024,), 3 * T)
        gather_plane(1, 0, (1024,), 4 * T)
        quantize(x_codes[0], x_scales[0], xg[0], 0, S)
        interleave(nc.vector.tensor_copy, 1, 0, 1024)
        quantize(x_codes[1], x_scales[1], xg[1], 0, S)

        w_grp, w_codes, w_scales = {}, {}, {}
        copies = {"s": nc.scalar.copy, "v": nc.vector.tensor_copy, "g": gpsimd_copy}

        def group_w(e):
            pool, tag = (swap, "slot_grp") if e == 3 else (keep, f"w_grp{e}")
            w_grp[e] = pool.tile([P, PASSES * N * 4], BF16, name=f"w_grp{e}", tag=tag, align_bytes=64)
            for c, a, n, engine in W_PLAN[e]:
                col = c * N + a
                copies[engine](
                    out=w_grp[e][:, 4 * col : 4 * (col + n)].rearrange("p (g i j) -> p g j i", i=4, j=4),
                    in_=w_raw[e, c][:, :, a : a + n].rearrange("p j (g i) -> p g j i", i=4),
                )

        def quantize_w(e):
            w_codes[e] = keep.tile([P, PASSES * N], U32, name=f"w_codes{e}", align_bytes=64)
            w_scales[e] = keep.tile([P, PASSES * N], U8, name=f"w_scales{e}", align_bytes=64)
            quantize(w_codes[e], w_scales[e], w_grp[e], 0, 512)
            quantize(w_codes[e], w_scales[e], w_grp[e], 512, 256)

        def product(acc, e, n, moving):
            for c in range(PASSES):
                cols = slice(c * N + n * P, c * N + (n + 1) * P)
                codes, scales = moving[c]
                nc.tensor.matmul_mx(
                    out=acc[:],
                    lhsT=w_codes[e][:, cols].bitcast(FP8X4),
                    lhsT_scale=w_scales[e][:, cols],
                    rhs=codes.bitcast(FP8X4),
                    rhs_scale=scales,
                    start=(c == 0),
                    stop=(c == PASSES - 1),
                )

        for e in range(E):
            group_w(e)
        for e in range(E):
            quantize_w(e)
        xs_codes = swap.tile([P, PASSES * T], U32, name="xs_codes", tag="slot_grp", align_bytes=64)
        xs_scales = keep.tile([P, PASSES * T], U8, name="xs_scales", align_bytes=64)
        quantize(xs_codes, xs_scales, xs, 0, 2 * T)
        y = []
        for n in range(N_TILES):
            y.append(swap.tile([P, S], F32, name=f"y{n}", tag=f"slot_y{n}", align_bytes=64))
            for e in range(E):
                slots = slice(e * C, (e + 1) * C)
                acc = psum.tile([P, C], F32, name="acc")
                product(acc, e, n, [(x_codes[c][:, slots], x_scales[c][:, slots]) for c in range(PASSES)])
                nc.scalar.activation(out=y[n][:, slots], in_=acc[:], func=RELU, bias=bias[:, n, e : e + 1], scale=1.0)

        mixed = []

        def combine(n):
            t1 = keep.tile([P, T], F32, name=f"t1_{n}")
            nc.vector.tensor_tensor(out=t1[:], in0=y[n][:].indirect(lists["pos1"][:]), in1=gates[n][:, 0, :], op=MULT)
            t2 = keep.tile([P, T], F32, name=f"t2_{n}")
            nc.vector.tensor_tensor(out=t2[:], in0=y[n][:].indirect(lists["pos2"][:]), in1=gates[n][:, 1, :], op=MULT)
            mixed.append(keep.tile([P, T], F32, name=f"mixed{n}"))
            nc.vector.scalar_tensor_tensor(
                out=mixed[n][:], in0=t1[:], scalar=bias[:, n, E : E + 1], in1=t2[:], op0=ADD, op1=ADD
            )

        combine(0)
        group_w(E)
        quantize_w(E)
        combine(1)
        combine(2)
        for n in range(N_TILES):
            acc = psum.tile([P, T], F32, name="acc")
            product(acc, E, n, [(xs_codes[:, c * T : (c + 1) * T], xs_scales[:, c * T : (c + 1) * T]) for c in range(PASSES)])
            res = keep.tile([P, T], F32, name=f"res{n}")
            nc.vector.scalar_tensor_tensor(
                out=res[:], in0=acc[:], scalar=neg_bias[:, n : n + 1], in1=mixed[n][:], op0=MAX, op1=ADD
            )
            nc.sync.dma_start(out=out[n * P : (n + 1) * P, :], in_=res[:])
